import numpy as np
import ml_dtypes


def mxq(x, axis, fmt="e4m3"):
    dtype, down = {"e4m3": (ml_dtypes.float8_e4m3fn, 7), "e5m2": (ml_dtypes.float8_e5m2, 14)}[fmt]
    v = np.moveaxis(np.asarray(x, np.float32).astype(ml_dtypes.bfloat16).astype(np.float64), axis, -1)
    blocks = v.reshape(v.shape[:-1] + (-1, 32))
    amax = np.abs(blocks).max(-1, keepdims=True)
    byte = np.maximum(np.where(amax > 0, np.frexp(amax)[1] - 1 + 127, 0) - down, 1)
    scale = np.exp2(byte - 127.0)
    codes = (blocks / scale).astype(np.float32).astype(dtype).astype(np.float64)
    return np.moveaxis((codes * scale).reshape(v.shape), -1, axis)


WIDE = False


def mx_kscale(k):
    if not WIDE:
        return np.ones(k)
    levels = np.array([10, -10, 5, -5, 0])
    if k % 512:
        return np.exp2(np.random.permutation(np.resize(levels, k // 32))).repeat(32)
    a = np.empty((k // 512, 16))
    for p in range(k // 512):
        a[p, :8] = np.random.permutation(np.resize(levels, 8))
        for g in range(8):
            far = levels[np.abs(levels - a[p, g]) >= 10]
            a[p, g + 8] = far[np.random.randint(len(far))]
    return np.exp2(a.ravel()).repeat(32)


def f64(x):
    return np.asarray(x).astype(np.float64)


def striped(idx):
    return np.tile(idx.reshape(-1, 16).T, (8, 1)).astype(np.uint16)


def unstriped(offs):
    return offs[:16].T.reshape(-1).astype(np.int64)


def striped8(idx):
    return np.concatenate([x.reshape(-1, 16).T for x in idx]).astype(np.uint16)


def runs(offs, k):
    lists = np.stack([offs[16 * r : 16 * r + 16].T.reshape(-1) for r in range(8)]).astype(np.int64)
    return lists[np.arange(k) % 512 // 64]


def pack_weight(w):
    k, n = w.shape
    w = f64(np.asarray(w, np.float32).astype(ml_dtypes.bfloat16)).reshape(k // 32, 32, n)
    amax = np.abs(w).max(1)
    byte = np.clip(np.where(amax > 0, np.frexp(amax)[1] - 1 + 127 - 7, 1), 1, 254)
    scaled = (w * np.exp2(127.0 - byte)[:, None, :]).reshape(k, n).astype(np.float32)
    words = np.ascontiguousarray(scaled.reshape(k // 512, 128, 4, n).transpose(0, 1, 3, 2)).astype(ml_dtypes.float8_e4m3fn).view(np.uint8)
    return words, np.ascontiguousarray(byte.astype(np.uint8).reshape(k // 512, 16, n))


def unpack_weight(words, scales):
    g, p, n, _ = words.shape
    vals = np.ascontiguousarray(words).view(ml_dtypes.float8_e4m3fn).astype(np.float64) * np.repeat(np.exp2(scales.astype(np.float64) - 127.0), 8, axis=1)[..., None]
    return vals.transpose(0, 1, 3, 2).reshape(g * 512, n)


def sigmoid(v):
    return 1.0 / (1.0 + np.exp(-np.maximum(v, -700.0)))


K, T, S, N, H, G, W = 512, 1024, 512, 512, 512, 2048, 384


def setup_inputs():
    n = np.random.standard_normal
    s = mx_kscale(K)[:, None]
    u = mx_kscale(S)
    packed_xT = pack_weight(n((K, T)) * s)
    packed_dT = pack_weight(n((K, G)) / s)
    return {
        "x_words": packed_xT[0],
        "x_scales": packed_xT[1],
        "w1": (n((K, H)) / np.sqrt(K) / s).astype(np.float32),
        "d_words": packed_dT[0],
        "d_scales": packed_dT[1],
        "gn": (np.random.uniform(0.5, 1.5, (H, 1)) * u[:, None]).astype(np.float32),
        "gk": (np.random.uniform(0.5, 1.5, (H, 1)) * u[:, None]).astype(np.float32),
        "w2": (n((H, N)) / np.sqrt(2 * H) / u[:, None]).astype(np.float32),
        "w3": (n((H, N)) / np.sqrt(2 * H) / u[:, None]).astype(np.float32),
        "sl": np.random.uniform(1.5, 3.0, (N, 1)).astype(np.float32),
        "th": (0.5 * n((N, 1))).astype(np.float32),
        "offs": striped(np.random.permutation(T)[:S]),
        "kidx": striped8(np.random.randint(0, G, (8, H))),
        "two": striped(np.random.permutation(T)[:S]),
        "n1": striped(np.random.permutation(S)),
        "n2": striped(np.random.permutation(S)),
        "n3": striped(np.random.permutation(S)[:W]),
        "n4": striped(np.random.permutation(S)[:W]),
        "n5": striped(np.random.permutation(S)),
        "n6": striped(np.random.permutation(S)),
    }


def reference(x_words, x_scales, w1, d_words, d_scales, gn, gk, w2, w3, sl, th, offs, kidx, two, n1, n2, n3, n4, n5, n6):
    xq = unpack_weight(x_words, x_scales)[:, unstriped(offs)]
    y = mxq(f64(w1), 0, "e4m3").T @ xq
    z = f64(gn) * (np.maximum(y[:, unstriped(n1)], y[:, unstriped(n2)]) - (0.75 * y))
    d_kidx = unpack_weight(d_words, d_scales)[np.arange(K)[:, None], runs(kidx, K)]
    x_two = unpack_weight(x_words, x_scales)[:, unstriped(two)]
    s = 0.0625 * (d_kidx.T @ x_two)
    old = s[:, unstriped(n3)]
    pa = s[:, unstriped(n4)]
    ra = old / (np.abs(pa) + 0.5)
    ds = s.copy()
    ds[:, unstriped(n3)] = ra
    z2 = f64(gk) * ds
    h = mxq(f64(w2), 0, "e4m3").T @ mxq(z, 0, "e4m3") + mxq(f64(w3), 0, "e4m3").T @ mxq(z2, 0, "e4m3")
    sg = sigmoid(f64(sl) * (h[:, unstriped(n5)] - f64(th)))
    return 1.5 * (h * (sg - sg[:, unstriped(n6)]))

@@ -1,0 +1,235 @@
+from contextlib import ExitStack
+
+import concourse.mybir as mybir
+
+F32 = mybir.dt.float32
+BF16 = mybir.dt.bfloat16
+I32 = mybir.dt.int32
+U32 = mybir.dt.uint32
+U16 = mybir.dt.uint16
+U8 = mybir.dt.uint8
+FP8X4 = mybir.dt.float8_e4m3fn_x4
+ALU = mybir.AluOpType
+ACT = mybir.ActivationFunctionType
+
+P = 128
+PACK = 4
+T, G, S, W = 1024, 2048, 512, 384
+SPARE = 16
+FLOPS = 4 * 2 * 512 * 512 * 512
+
+
+def tile_picked_jkeyoverknormedb_none_p_kernel(
+    tc, x_words, x_scales, w1, d_words, d_scales, gn, gk, w2, w3, sl, th,
+    offs, kidx, two, n1, n2, n3, n4, n5, n6, out,
+):
+    nc = tc.nc
+    with ExitStack() as ctx:
+        lists = ctx.enter_context(tc.tile_pool(name="lists", bufs=1))
+        keep = ctx.enter_context(tc.tile_pool(name="keep", bufs=1))
+        psum = ctx.enter_context(tc.psum_pool(name="psum", bufs=1))
+
+        def sb(name, shape, dtype, tag=None):
+            return keep.tile(shape, dtype, name=name, tag=tag or name, align_bytes=64)
+
+        def load_list(name, ap):
+            tile = lists.tile(list(ap.shape), U16, name=name)
+            nc.sync.dma_start(tile[:], ap)
+            return tile
+
+        def load_column(name, ap):
+            tile = sb(name, [P, PACK], F32)
+            nc.sync.dma_start(tile[:], ap.rearrange("(p t) o -> p (t o)", t=PACK))
+            return tile
+
+        def load_weight(name, w, pieces):
+            width = S // pieces
+            rows = w.rearrange("(p j) c -> p j c", j=PACK)
+            tiles = []
+            for h in range(pieces):
+                raw = sb("%s_raw%d" % (name, h), [P, PACK, width], F32)
+                nc.sync.dma_start(raw[:], rows[:, :, h * width : (h + 1) * width])
+                tiles.append(raw)
+            return tiles
+
+        def load_half(name, w, h, queue):
+            width = S // 2
+            rows = w.rearrange("(p j) c -> p j c", j=PACK)
+            raw = sb("%s_raw%d" % (name, h), [P, PACK, width], F32)
+            queue.dma_start(raw[:], rows[:, :, h * width : (h + 1) * width])
+            return raw
+
+        def round_weight(name, raws, copies, tag=None):
+            grouped = sb(name + "_bf16", [P, PACK * S], BF16, tag)
+            view = grouped[:].rearrange("p (t m j) -> p m t j", t=PACK, j=PACK)
+            step = P // len(raws)
+            for h, (raw, copy) in enumerate(zip(raws, copies)):
+                copy(view[:, h * step : (h + 1) * step], raw[:].rearrange("p j (m t) -> p m t j", t=PACK))
+            return grouped
+
+        def quantize(name, grouped):
+            codes = sb(name + "_codes", [P, S], U32)
+            scales = sb(name + "_scales", [P, S], U8)
+            nc.vector.quantize_mx(out=codes[:].bitcast(FP8X4), scales=scales[:], in_=grouped[:])
+            return codes, scales
+
+        def gather(name, window, offsets, dtype):
+            picked = sb(name, [P, S], dtype)
+            nc.vector.tensor_copy(picked[:], window.indirect(offsets[:]))
+            return picked
+
+        def product(bank, lhs, t, rhs, start, stop):
+            cols = slice(t * P, (t + 1) * P)
+            nc.tensor.matmul_mx(
+                out=bank[:],
+                lhsT=lhs[0][:, cols].bitcast(FP8X4), lhsT_scale=lhs[1][:, cols],
+                rhs=rhs[0][:].bitcast(FP8X4), rhs_scale=rhs[1][:],
+                start=start, stop=stop,
+            )
+
+        def interleave(name, planes, copies, widths):
+            grouped = sb(name, [P, PACK * S], BF16)
+            target = grouped[:].rearrange("p (c t) -> p c t", t=PACK)
+            source = planes[:].rearrange("p t c -> p c t")
+            start = 0
+            for copy, width in zip(copies, widths):
+                copy(target[:, start : start + width], source[:, start : start + width])
+                start = start + width
+            return grouped
+
+        x_bytes = sb("x_bytes", [P, T], U8)
+        d_bytes = sb("d_bytes", [P, G], U8)
+        nc.vector.memset(d_bytes[:].bitcast(I32), 0)
+        nc.vector.memset(x_bytes[:].bitcast(I32), 0)
+
+        kidx_t = load_list("kidx_t", kidx)
+        for r in range(2):
+            nc.sync.dma_start(d_bytes[r:P:16, :].bitcast(I32), d_scales[0][r:16:2, :].bitcast(I32))
+        for r in range(4):
+            nc.sync.dma_start(x_bytes[r:P:32, :].bitcast(I32), x_scales[0][r:16:4, :].bitcast(I32))
+        x_table = sb("x_table", [P, T], I32)
+        nc.sync.dma_start(x_table[:], x_words[0].rearrange("p c r -> p (c r)").bitcast(I32))
+        two_t = load_list("two_t", two)
+        d_table = sb("d_table", [P, G], I32)
+        nc.sync.dma_start(d_table[:], d_words[0].rearrange("p c r -> p (c r)").bitcast(I32))
+        offs_t = load_list("offs_t", offs)
+        w1_raw = load_weight("w1", w1, 2)
+
+        y_rows = [sb("y_rows%d" % t, [P, S + SPARE], F32) for t in range(PACK)]
+        sg_rows = [sb("sg_rows%d" % t, [P, S + SPARE], F32) for t in range(PACK)]
+        for tile in y_rows + sg_rows:
+            nc.vector.memset(tile[:, S:], 0.0)
+        h_rows = [sb("h_rows%d" % t, [P, 2 * S], F32) for t in range(PACK)]
+
+        key_bytes = gather("key_bytes", d_bytes[:], kidx_t, U8)
+        key_dealt = sb("key_dealt", [P, S], U8)
+        nc.vector.tensor_copy(
+            key_dealt[:].rearrange("p (t m) -> p m t", t=PACK), key_bytes[:].rearrange("p (m t) -> p m t", t=PACK)
+        )
+        key_scales = sb("key_scales", [P, S], U8)
+        nc.vector.tensor_copy(key_scales[:].bitcast(I32), key_dealt[:].bitcast(I32))
+        for r in range(2):
+            nc.sync.dma_start(key_scales[2 + r : P : 32, :].bitcast(I32), key_dealt[16 + r : P : 32, :].bitcast(I32))
+
+        n4_t = load_list("n4_t", n4)
+        n3_t = load_list("n3_t", n3)
+        w3_raw = load_weight("w3", w3, 1)
+        w2_raw = load_weight("w2", w2, 1)
+        n1_t = load_list("n1_t", n1)
+        n2_t = load_list("n2_t", n2)
+        gn_t = load_column("gn_t", gn)
+        gk_t = load_column("gk_t", gk)
+        sl_t = load_column("sl_t", sl)
+        th_t = load_column("th_t", th)
+        n5_t = load_list("n5_t", n5)
+        n6_t = load_list("n6_t", n6)
+
+        x_view = x_table[:].bitcast(U32)
+        x2_codes = gather("x2_codes", x_view, two_t, U32)
+        x2_scales = gather("x2_scales", x_bytes[:], two_t, U8)
+        key_words = gather("key_words", d_table[:].bitcast(U32), kidx_t, U32)
+        key_codes = sb("key_codes", [P, S], U32)
+        nc.vector.tensor_copy(
+            key_codes[:].rearrange("p (t m) -> p m t", t=PACK), key_words[:].rearrange("p (m t) -> p m t", t=PACK)
+        )
+        xq_codes = gather("xq_codes", x_view, offs_t, U32)
+        xq_scales = gather("xq_scales", x_bytes[:], offs_t, U8)
+        w1_q = quantize("w1", round_weight("w1", w1_raw, [nc.scalar.copy] * 2))
+
+        w3_q = quantize("w3", round_weight("w3", w3_raw, [nc.vector.tensor_copy]))
+        w2_q = quantize("w2", round_weight("w2", w2_raw, [nc.vector.tensor_copy]))
+        gn_neg = sb("gn_neg", [P, PACK], F32)
+        nc.vector.tensor_scalar(gn_neg[:], gn_t[:], -0.75, None, ALU.mult)
+        bias = sb("bias", [P, PACK], F32)
+        nc.vector.scalar_tensor_tensor(bias[:], th_t[:], -1.0, sl_t[:], ALU.mult, ALU.mult)
+
+        z_planes = sb("z_planes", [P, PACK, S], BF16)
+        z2_planes = sb("z2_planes", [P, PACK, S], BF16)
+
+        def make_z(t):
+            bank = psum.tile([P, S], F32, name="y_bank%d" % t, tag="shared%d" % [1, 2, 3, 2][t])
+            product(bank, w1_q, t, (xq_codes, xq_scales), True, True)
+            nc.scalar.copy(y_rows[t][:, :S], bank[:])
+            first = sb("first%d" % t, [P, S], F32)
+            second = sb("second%d" % t, [P, S], F32)
+            nc.scalar.activation(first[:], y_rows[t][:].indirect(n1_t[:]), ACT.Copy)
+            nc.scalar.activation(second[:], y_rows[t][:].indirect(n2_t[:]), ACT.Copy)
+            own = h_rows[t][:, S:]
+            nc.scalar.activation(own, bank[:], ACT.Copy, scale=gn_neg[:, t : t + 1])
+            larger = sb("larger%d" % t, [P, S], F32)
+            nc.vector.tensor_tensor(larger[:], first[:], second[:], ALU.max)
+            nc.vector.scalar_tensor_tensor(z_planes[:, t, :], larger[:], gn_t[:, t : t + 1], own, ALU.mult, ALU.add)
+
+        def make_z2(t):
+            bank = psum.tile([P, S], F32, name="s_bank%d" % t, tag="shared%d" % t)
+            product(bank, (key_codes, key_scales), t, (x2_codes, x2_scales), True, True)
+            s_rows = sb("s_rows%d" % t, [P, S], F32, [None, None, "size0", "size1"][t])
+            nc.scalar.activation(s_rows[:], bank[:], ACT.Copy, scale=0.0625)
+            pa = sb("pa%d" % t, [P, W], F32)
+            nc.scalar.activation(pa[:], s_rows[:].indirect(n4_t[:]), ACT.Copy)
+            size = sb("size%d" % t, [P, W], F32)
+            nc.scalar.activation(size[:], pa[:], ACT.Abs)
+            root = sb("root%d" % t, [P, W], F32)
+            nc.scalar.activation(root[:], size[:], ACT.Abs_reciprocal_sqrt, bias=0.5)
+            half = sb("half%d" % t, [P, W], F32)
+            nc.vector.tensor_tensor(half[:], s_rows[:].indirect(n3_t[:]), root[:], ALU.mult)
+            nc.vector.tensor_tensor(s_rows[:].indirect(n3_t[:]), half[:], root[:], ALU.mult)
+            nc.vector.tensor_scalar(z2_planes[:, t, :], s_rows[:], gk_t[:, t : t + 1], None, ALU.mult)
+
+        make_z2(0)
+        make_z2(1)
+        make_z(0)
+        make_z2(2)
+        make_z2(3)
+        for t in range(1, PACK):
+            make_z(t)
+        z2_q = quantize("z2", interleave("z2_bf16", z2_planes, [nc.scalar.copy], [S]))
+        z_q = quantize("z", interleave("z_bf16", z_planes, [nc.vector.tensor_copy, nc.scalar.copy], [320, 192]))
+        h_banks = [psum.tile([P, S], F32, name="h_bank%d" % t, tag="last%d" % t) for t in range(PACK)]
+
+        out_rows = out.rearrange("(p t) j -> p t j", t=PACK)
+        for t in range(PACK):
+            product(h_banks[t], w3_q, t, z2_q, True, False)
+            product(h_banks[t], w2_q, t, z_q, False, True)
+        for t in range(PACK):
+            h = h_rows[t][:, :S]
+            nc.vector.tensor_copy(h, h_banks[t][:])
+            sg = sg_rows[t][:, :S]
+            nc.scalar.activation(
+                sg, h_rows[t][:].indirect(n5_t[:]), ACT.Sigmoid, bias=bias[:, t : t + 1], scale=sl_t[:, t : t + 1]
+            )
+            diff = sb("diff%d" % t, [P, S], F32)
+            if t < PACK - 1:
+                minus = sb("minus%d" % t, [P, S], F32)
+                if t == 0:
+                    nc.vector.tensor_scalar(minus[:], sg, -1.0, None, ALU.mult)
+                else:
+                    nc.scalar.activation(minus[:], sg, ACT.Copy, scale=-1.0)
+                nc.vector.tensor_tensor(diff[:], sg_rows[t][:].indirect(n6_t[:]), minus[:], ALU.add)
+            else:
+                other = sb("other%d" % t, [P, S], F32)
+                nc.scalar.activation(other[:], sg_rows[t][:].indirect(n6_t[:]), ACT.Copy)
+                nc.vector.tensor_tensor(diff[:], other[:], sg, ALU.subtract)
+            result = sb("result%d" % t, [P, S], F32)
+            nc.vector.scalar_tensor_tensor(result[:], h, -1.5, diff[:], ALU.mult, ALU.mult)
+            nc.sync.dma_start(out_rows[:, t, :], result[:])

@@ -101,19 +101,19 @@ def tile_picked_jkeyoverknormedb_none_p_kernel(
         d_bytes = sb("d_bytes", [P, G], U8)
         nc.vector.memset(d_bytes[:].bitcast(I32), 0)
         nc.vector.memset(x_bytes[:].bitcast(I32), 0)
+        key_rows = sb("key_rows", [P, S], U8)
+        nc.vector.memset(key_rows[:].bitcast(I32), 0)
 
         kidx_t = load_list("kidx_t", kidx)
         for r in range(2):
             nc.sync.dma_start(d_bytes[r:P:16, :].bitcast(I32), d_scales[0][r:16:2, :].bitcast(I32))
-        for r in range(4):
-            nc.sync.dma_start(x_bytes[r:P:32, :].bitcast(I32), x_scales[0][r:16:4, :].bitcast(I32))
+        two_t = load_list("two_t", two)
         x_table = sb("x_table", [P, T], I32)
         nc.sync.dma_start(x_table[:], x_words[0].rearrange("p c r -> p (c r)").bitcast(I32))
-        two_t = load_list("two_t", two)
+        for r in range(4):
+            nc.sync.dma_start(x_bytes[r:P:32, :].bitcast(I32), x_scales[0][r:16:4, :].bitcast(I32))
         d_table = sb("d_table", [P, G], I32)
         nc.sync.dma_start(d_table[:], d_words[0].rearrange("p c r -> p (c r)").bitcast(I32))
-        offs_t = load_list("offs_t", offs)
-        w1_raw = load_weight("w1", w1, 2)
 
         y_rows = [sb("y_rows%d" % t, [P, S + SPARE], F32) for t in range(PACK)]
         sg_rows = [sb("sg_rows%d" % t, [P, S + SPARE], F32) for t in range(PACK)]
@@ -122,23 +122,23 @@ def tile_picked_jkeyoverknormedb_none_p_kernel(
         h_rows = [sb("h_rows%d" % t, [P, 2 * S], F32) for t in range(PACK)]
 
         key_bytes = gather("key_bytes", d_bytes[:], kidx_t, U8)
-        key_dealt = sb("key_dealt", [P, S], U8)
-        nc.vector.tensor_copy(
-            key_dealt[:].rearrange("p (t m) -> p m t", t=PACK), key_bytes[:].rearrange("p (m t) -> p m t", t=PACK)
-        )
+        for r in range(4):
+            source = 16 * (r // 2) + r % 2
+            nc.sync.dma_start(key_rows[r:P:32, :].bitcast(I32), key_bytes[source:P:32, :].bitcast(I32))
         key_scales = sb("key_scales", [P, S], U8)
-        nc.vector.tensor_copy(key_scales[:].bitcast(I32), key_dealt[:].bitcast(I32))
-        for r in range(2):
-            nc.sync.dma_start(key_scales[2 + r : P : 32, :].bitcast(I32), key_dealt[16 + r : P : 32, :].bitcast(I32))
-
+        nc.vector.tensor_copy(
+            key_scales[:].rearrange("p (t m) -> p m t", t=PACK), key_rows[:].rearrange("p (m t) -> p m t", t=PACK)
+        )
+        offs_t = load_list("offs_t", offs)
+        w1_raw = load_weight("w1", w1, 2)
+        w3_raw = load_weight("w3", w3, 1)
         n4_t = load_list("n4_t", n4)
         n3_t = load_list("n3_t", n3)
-        w3_raw = load_weight("w3", w3, 1)
-        w2_raw = load_weight("w2", w2, 1)
         n1_t = load_list("n1_t", n1)
         n2_t = load_list("n2_t", n2)
         gn_t = load_column("gn_t", gn)
         gk_t = load_column("gk_t", gk)
+        w2_raw = load_weight("w2", w2, 1)
         sl_t = load_column("sl_t", sl)
         th_t = load_column("th_t", th)
         n5_t = load_list("n5_t", n5)
@@ -157,9 +157,8 @@ def tile_picked_jkeyoverknormedb_none_p_kernel(
         w1_q = quantize("w1", round_weight("w1", w1_raw, [nc.scalar.copy] * 2))
 
         w3_q = quantize("w3", round_weight("w3", w3_raw, [nc.vector.tensor_copy]))
-        w2_q = quantize("w2", round_weight("w2", w2_raw, [nc.vector.tensor_copy]))
         gn_neg = sb("gn_neg", [P, PACK], F32)
-        nc.vector.tensor_scalar(gn_neg[:], gn_t[:], -0.75, None, ALU.mult)
+        nc.scalar.activation(gn_neg[:], gn_t[:], ACT.Copy, scale=-0.75)
         bias = sb("bias", [P, PACK], F32)
         nc.vector.scalar_tensor_tensor(bias[:], th_t[:], -1.0, sl_t[:], ALU.mult, ALU.mult)
 
@@ -167,7 +166,7 @@ def tile_picked_jkeyoverknormedb_none_p_kernel(
         z2_planes = sb("z2_planes", [P, PACK, S], BF16)
 
         def make_z(t):
-            bank = psum.tile([P, S], F32, name="y_bank%d" % t, tag="shared%d" % [1, 2, 3, 2][t])
+            bank = psum.tile([P, S], F32, name="y_bank%d" % t, tag="shared%d" % [2, 3, 2, 3][t])
             product(bank, w1_q, t, (xq_codes, xq_scales), True, True)
             nc.scalar.copy(y_rows[t][:, :S], bank[:])
             first = sb("first%d" % t, [P, S], F32)
@@ -183,7 +182,7 @@ def tile_picked_jkeyoverknormedb_none_p_kernel(
         def make_z2(t):
             bank = psum.tile([P, S], F32, name="s_bank%d" % t, tag="shared%d" % t)
             product(bank, (key_codes, key_scales), t, (x2_codes, x2_scales), True, True)
-            s_rows = sb("s_rows%d" % t, [P, S], F32, [None, None, "size0", "size1"][t])
+            s_rows = sb("s_rows%d" % t, [P, S], F32, ["w1_raw0", "size0", "pa0", "size2"][t])
             nc.scalar.activation(s_rows[:], bank[:], ACT.Copy, scale=0.0625)
             pa = sb("pa%d" % t, [P, W], F32)
             nc.scalar.activation(pa[:], s_rows[:].indirect(n4_t[:]), ACT.Copy)
@@ -198,12 +197,13 @@ def tile_picked_jkeyoverknormedb_none_p_kernel(
 
         make_z2(0)
         make_z2(1)
-        make_z(0)
         make_z2(2)
+        make_z(0)
         make_z2(3)
+        z2_q = quantize("z2", interleave("z2_bf16", z2_planes, [nc.vector.tensor_copy], [S]))
         for t in range(1, PACK):
             make_z(t)
-        z2_q = quantize("z2", interleave("z2_bf16", z2_planes, [nc.scalar.copy], [S]))
+        w2_q = quantize("w2", round_weight("w2", w2_raw, [nc.scalar.copy], "y_rows3"))
         z_q = quantize("z", interleave("z_bf16", z_planes, [nc.vector.tensor_copy, nc.scalar.copy], [320, 192]))
         h_banks = [psum.tile([P, S], F32, name="h_bank%d" % t, tag="last%d" % t) for t in range(PACK)]
 
@@ -231,5 +231,8 @@ def tile_picked_jkeyoverknormedb_none_p_kernel(
                 nc.scalar.activation(other[:], sg_rows[t][:].indirect(n6_t[:]), ACT.Copy)
                 nc.vector.tensor_tensor(diff[:], other[:], sg, ALU.subtract)
             result = sb("result%d" % t, [P, S], F32)
-            nc.vector.scalar_tensor_tensor(result[:], h, -1.5, diff[:], ALU.mult, ALU.mult)
-            nc.sync.dma_start(out_rows[:, t, :], result[:])
+            pieces = 2 if t == PACK - 1 else 1
+            for piece in range(pieces):
+                cols = slice(piece * S // pieces, (piece + 1) * S // pieces)
+                nc.vector.scalar_tensor_tensor(result[:, cols], h[:, cols], -1.5, diff[:, cols], ALU.mult, ALU.mult)
+                nc.sync.dma_start(out_rows[:, t, cols], result[:, cols])

@@ -119,6 +119,9 @@ def tile_picked_jkeyoverknormedb_none_p_kernel(
         sg_rows = [sb("sg_rows%d" % t, [P, S + SPARE], F32) for t in range(PACK)]
         for tile in y_rows + sg_rows:
             nc.vector.memset(tile[:, S:], 0.0)
+        warm = sb("warm", [P, 16], F32)
+        nc.gpsimd.memset(warm[:, 0:1], 0.0)
+        nc.scalar.activation(warm[:, 8:9], warm[:, 0:1], ACT.Abs_reciprocal_sqrt, bias=0.5)
         h_rows = [sb("h_rows%d" % t, [P, 2 * S], F32) for t in range(PACK)]
 
         key_bytes = gather("key_bytes", d_bytes[:], kidx_t, U8)

@@ -61,10 +61,10 @@ def tile_picked_jkeyoverknormedb_none_p_kernel(
 
         def round_weight(name, raws, copies, tag=None):
             grouped = sb(name + "_bf16", [P, PACK * S], BF16, tag)
-            view = grouped[:].rearrange("p (t m j) -> p m t j", t=PACK, j=PACK)
+            view = grouped[:].rearrange("p (t m j) -> p m j t", t=PACK, j=PACK)
             step = P // len(raws)
             for h, (raw, copy) in enumerate(zip(raws, copies)):
-                copy(view[:, h * step : (h + 1) * step], raw[:].rearrange("p j (m t) -> p m t j", t=PACK))
+                copy(view[:, h * step : (h + 1) * step], raw[:].rearrange("p j (m t) -> p m j t", t=PACK))
             return grouped
 
         def quantize(name, grouped):
@@ -89,8 +89,8 @@ def tile_picked_jkeyoverknormedb_none_p_kernel(
 
         def interleave(name, planes, copies, widths):
             grouped = sb(name, [P, PACK * S], BF16)
-            target = grouped[:].rearrange("p (c t) -> p c t", t=PACK)
-            source = planes[:].rearrange("p t c -> p c t")
+            target = grouped[:].rearrange("p (c i t) -> p c t i", t=PACK, i=PACK)
+            source = planes[:].rearrange("p t (c i) -> p c t i", i=PACK)
             start = 0
             for copy, width in zip(copies, widths):
                 copy(target[:, start : start + width], source[:, start : start + width])
@@ -203,11 +203,11 @@ def tile_picked_jkeyoverknormedb_none_p_kernel(
         make_z2(2)
         make_z(0)
         make_z2(3)
-        z2_q = quantize("z2", interleave("z2_bf16", z2_planes, [nc.vector.tensor_copy], [S]))
+        z2_q = quantize("z2", interleave("z2_bf16", z2_planes, [nc.vector.tensor_copy], [S // PACK]))
         for t in range(1, PACK):
             make_z(t)
         w2_q = quantize("w2", round_weight("w2", w2_raw, [nc.scalar.copy], "y_rows3"))
-        z_q = quantize("z", interleave("z_bf16", z_planes, [nc.vector.tensor_copy, nc.scalar.copy], [320, 192]))
+        z_q = quantize("z", interleave("z_bf16", z_planes, [nc.vector.tensor_copy, nc.scalar.copy], [80, 48]))
         h_banks = [psum.tile([P, S], F32, name="h_bank%d" % t, tag="last%d" % t) for t in range(PACK)]
 
         out_rows = out.rearrange("(p t) j -> p t j", t=PACK)

@@ -185,7 +185,7 @@ def tile_picked_jkeyoverknormedb_none_p_kernel(
         def make_z2(t):
             bank = psum.tile([P, S], F32, name="s_bank%d" % t, tag="shared%d" % t)
             product(bank, (key_codes, key_scales), t, (x2_codes, x2_scales), True, True)
-            s_rows = sb("s_rows%d" % t, [P, S], F32, ["w1_raw0", "size0", "pa0", "size2"][t])
+            s_rows = sb("s_rows%d" % t, [P, S], F32, ["w1_raw0", "pa0", "size0", "size1"][t])
             nc.scalar.activation(s_rows[:], bank[:], ACT.Copy, scale=0.0625)
             pa = sb("pa%d" % t, [P, W], F32)
             nc.scalar.activation(pa[:], s_rows[:].indirect(n4_t[:]), ACT.Copy)
@@ -207,7 +207,7 @@ def tile_picked_jkeyoverknormedb_none_p_kernel(
         for t in range(1, PACK):
             make_z(t)
         w2_q = quantize("w2", round_weight("w2", w2_raw, [nc.scalar.copy], "y_rows3"))
-        z_q = quantize("z", interleave("z_bf16", z_planes, [nc.vector.tensor_copy, nc.scalar.copy], [80, 48]))
+        z_q = quantize("z", interleave("z_bf16", z_planes, [nc.vector.tensor_copy], [S // PACK]))
         h_banks = [psum.tile([P, S], F32, name="h_bank%d" % t, tag="last%d" % t) for t in range(PACK)]
 
         out_rows = out.rearrange("(p t) j -> p t j", t=PACK)
@@ -222,20 +222,19 @@ def tile_picked_jkeyoverknormedb_none_p_kernel(
                 sg, h_rows[t][:].indirect(n5_t[:]), ACT.Sigmoid, bias=bias[:, t : t + 1], scale=sl_t[:, t : t + 1]
             )
             diff = sb("diff%d" % t, [P, S], F32)
-            if t < PACK - 1:
+            result = sb("result%d" % t, [P, S], F32)
+            pieces = 2 if t == PACK - 1 else 1
+            if t < 2:
                 minus = sb("minus%d" % t, [P, S], F32)
-                if t == 0:
-                    nc.vector.tensor_scalar(minus[:], sg, -1.0, None, ALU.mult)
-                else:
-                    nc.scalar.activation(minus[:], sg, ACT.Copy, scale=-1.0)
+                nc.vector.tensor_scalar(minus[:], sg, -1.0, None, ALU.mult)
                 nc.vector.tensor_tensor(diff[:], sg_rows[t][:].indirect(n6_t[:]), minus[:], ALU.add)
             else:
                 other = sb("other%d" % t, [P, S], F32)
-                nc.scalar.activation(other[:], sg_rows[t][:].indirect(n6_t[:]), ACT.Copy)
-                nc.vector.tensor_tensor(diff[:], other[:], sg, ALU.subtract)
-            result = sb("result%d" % t, [P, S], F32)
-            pieces = 2 if t == PACK - 1 else 1
             for piece in range(pieces):
                 cols = slice(piece * S // pieces, (piece + 1) * S // pieces)
+                if t >= 2:
+                    entries = n6_t[:, cols.start // 16 : cols.stop // 16]
+                    nc.scalar.activation(other[:, cols], sg_rows[t][:].indirect(entries), ACT.Copy)
+                    nc.vector.tensor_tensor(diff[:, cols], other[:, cols], sg[:, cols], ALU.subtract)
                 nc.vector.scalar_tensor_tensor(result[:, cols], h[:, cols], -1.5, diff[:, cols], ALU.mult, ALU.mult)
                 nc.sync.dma_start(out_rows[:, t, cols], result[:, cols])

from contextlib import ExitStack

import concourse.mybir as mybir

F32 = mybir.dt.float32
BF16 = mybir.dt.bfloat16
I32 = mybir.dt.int32
U32 = mybir.dt.uint32
U16 = mybir.dt.uint16
U8 = mybir.dt.uint8
FP8X4 = mybir.dt.float8_e4m3fn_x4
ALU = mybir.AluOpType
ACT = mybir.ActivationFunctionType

P = 128
PACK = 4
T, G, S, W = 1024, 2048, 512, 384
SPARE = 16
FLOPS = 4 * 2 * 512 * 512 * 512


def tile_picked_jkeyoverknormedb_none_p_kernel(
    tc, x_words, x_scales, w1, d_words, d_scales, gn, gk, w2, w3, sl, th,
    offs, kidx, two, n1, n2, n3, n4, n5, n6, out,
):
    nc = tc.nc
    with ExitStack() as ctx:
        lists = ctx.enter_context(tc.tile_pool(name="lists", bufs=1))
        keep = ctx.enter_context(tc.tile_pool(name="keep", bufs=1))
        psum = ctx.enter_context(tc.psum_pool(name="psum", bufs=1))

        def sb(name, shape, dtype, tag=None):
            return keep.tile(shape, dtype, name=name, tag=tag or name, align_bytes=64)

        def load_list(name, ap):
            tile = lists.tile(list(ap.shape), U16, name=name)
            nc.sync.dma_start(tile[:], ap)
            return tile

        def load_column(name, ap):
            tile = sb(name, [P, PACK], F32)
            nc.sync.dma_start(tile[:], ap.rearrange("(p t) o -> p (t o)", t=PACK))
            return tile

        def load_weight(name, w, pieces):
            width = S // pieces
            rows = w.rearrange("(p j) c -> p j c", j=PACK)
            tiles = []
            for h in range(pieces):
                raw = sb("%s_raw%d" % (name, h), [P, PACK, width], F32)
                nc.sync.dma_start(raw[:], rows[:, :, h * width : (h + 1) * width])
                tiles.append(raw)
            return tiles

        def load_half(name, w, h, queue):
            width = S // 2
            rows = w.rearrange("(p j) c -> p j c", j=PACK)
            raw = sb("%s_raw%d" % (name, h), [P, PACK, width], F32)
            queue.dma_start(raw[:], rows[:, :, h * width : (h + 1) * width])
            return raw

        def round_weight(name, raws, copies, tag=None):
            grouped = sb(name + "_bf16", [P, PACK * S], BF16, tag)
            view = grouped[:].rearrange("p (t m j) -> p m j t", t=PACK, j=PACK)
            step = P // len(raws)
            for h, (raw, copy) in enumerate(zip(raws, copies)):
                copy(view[:, h * step : (h + 1) * step], raw[:].rearrange("p j (m t) -> p m j t", t=PACK))
            return grouped

        def quantize(name, grouped):
            codes = sb(name + "_codes", [P, S], U32)
            scales = sb(name + "_scales", [P, S], U8)
            nc.vector.quantize_mx(out=codes[:].bitcast(FP8X4), scales=scales[:], in_=grouped[:])
            return codes, scales

        def gather(name, window, offsets, dtype):
            picked = sb(name, [P, S], dtype)
            nc.vector.tensor_copy(picked[:], window.indirect(offsets[:]))
            return picked

        def product(bank, lhs, t, rhs, start, stop):
            cols = slice(t * P, (t + 1) * P)
            nc.tensor.matmul_mx(
                out=bank[:],
                lhsT=lhs[0][:, cols].bitcast(FP8X4), lhsT_scale=lhs[1][:, cols],
                rhs=rhs[0][:].bitcast(FP8X4), rhs_scale=rhs[1][:],
                start=start, stop=stop,
            )

        def interleave(name, planes, copies, widths):
            grouped = sb(name, [P, PACK * S], BF16)
            target = grouped[:].rearrange("p (c i t) -> p c t i", t=PACK, i=PACK)
            source = planes[:].rearrange("p t (c i) -> p c t i", i=PACK)
            start = 0
            for copy, width in zip(copies, widths):
                copy(target[:, start : start + width], source[:, start : start + width])
                start = start + width
            return grouped

        x_bytes = sb("x_bytes", [P, T], U8)
        d_bytes = sb("d_bytes", [P, G], U8)
        nc.vector.memset(d_bytes[:].bitcast(I32), 0)
        nc.vector.memset(x_bytes[:].bitcast(I32), 0)
        key_rows = sb("key_rows", [P, S], U8)
        nc.vector.memset(key_rows[:].bitcast(I32), 0)

        kidx_t = load_list("kidx_t", kidx)
        for r in range(2):
            nc.sync.dma_start(d_bytes[r:P:16, :].bitcast(I32), d_scales[0][r:16:2, :].bitcast(I32))
        two_t = load_list("two_t", two)
        x_table = sb("x_table", [P, T], I32)
        nc.sync.dma_start(x_table[:], x_words[0].rearrange("p c r -> p (c r)").bitcast(I32))
        for r in range(4):
            nc.sync.dma_start(x_bytes[r:P:32, :].bitcast(I32), x_scales[0][r:16:4, :].bitcast(I32))
        d_table = sb("d_table", [P, G], I32)
        nc.sync.dma_start(d_table[:], d_words[0].rearrange("p c r -> p (c r)").bitcast(I32))

        y_rows = [sb("y_rows%d" % t, [P, S + SPARE], F32) for t in range(PACK)]
        sg_rows = [sb("sg_rows%d" % t, [P, S + SPARE], F32) for t in range(PACK)]
        for tile in y_rows + sg_rows:
            nc.vector.memset(tile[:, S:], 0.0)
        warm = sb("warm", [P, 16], F32)
        nc.gpsimd.memset(warm[:, 0:1], 0.0)
        nc.scalar.activation(warm[:, 8:9], warm[:, 0:1], ACT.Abs_reciprocal_sqrt, bias=0.5)
        h_rows = [sb("h_rows%d" % t, [P, 2 * S], F32) for t in range(PACK)]

        key_bytes = gather("key_bytes", d_bytes[:], kidx_t, U8)
        for r in range(4):
            source = 16 * (r // 2) + r % 2
            nc.sync.dma_start(key_rows[r:P:32, :].bitcast(I32), key_bytes[source:P:32, :].bitcast(I32))
        key_scales = sb("key_scales", [P, S], U8)
        nc.vector.tensor_copy(
            key_scales[:].rearrange("p (t m) -> p m t", t=PACK), key_rows[:].rearrange("p (m t) -> p m t", t=PACK)
        )
        offs_t = load_list("offs_t", offs)
        w1_raw = load_weight("w1", w1, 2)
        w3_raw = load_weight("w3", w3, 1)
        n4_t = load_list("n4_t", n4)
        n3_t = load_list("n3_t", n3)
        n1_t = load_list("n1_t", n1)
        n2_t = load_list("n2_t", n2)
        gn_t = load_column("gn_t", gn)
        gk_t = load_column("gk_t", gk)
        w2_raw = load_weight("w2", w2, 1)
        sl_t = load_column("sl_t", sl)
        th_t = load_column("th_t", th)
        n5_t = load_list("n5_t", n5)
        n6_t = load_list("n6_t", n6)

        x_view = x_table[:].bitcast(U32)
        x2_codes = gather("x2_codes", x_view, two_t, U32)
        x2_scales = gather("x2_scales", x_bytes[:], two_t, U8)
        key_words = gather("key_words", d_table[:].bitcast(U32), kidx_t, U32)
        key_codes = sb("key_codes", [P, S], U32)
        nc.vector.tensor_copy(
            key_codes[:].rearrange("p (t m) -> p m t", t=PACK), key_words[:].rearrange("p (m t) -> p m t", t=PACK)
        )
        xq_codes = gather("xq_codes", x_view, offs_t, U32)
        xq_scales = gather("xq_scales", x_bytes[:], offs_t, U8)
        w1_q = quantize("w1", round_weight("w1", w1_raw, [nc.scalar.copy] * 2))

        w3_q = quantize("w3", round_weight("w3", w3_raw, [nc.vector.tensor_copy]))
        gn_neg = sb("gn_neg", [P, PACK], F32)
        nc.scalar.activation(gn_neg[:], gn_t[:], ACT.Copy, scale=-0.75)
        bias = sb("bias", [P, PACK], F32)
        nc.vector.scalar_tensor_tensor(bias[:], th_t[:], -1.0, sl_t[:], ALU.mult, ALU.mult)

        z_planes = sb("z_planes", [P, PACK, S], BF16)
        z2_planes = sb("z2_planes", [P, PACK, S], BF16)

        def make_z(t):
            bank = psum.tile([P, S], F32, name="y_bank%d" % t, tag="shared%d" % [2, 3, 2, 3][t])
            product(bank, w1_q, t, (xq_codes, xq_scales), True, True)
            nc.scalar.copy(y_rows[t][:, :S], bank[:])
            first = sb("first%d" % t, [P, S], F32)
            second = sb("second%d" % t, [P, S], F32)
            nc.scalar.activation(first[:], y_rows[t][:].indirect(n1_t[:]), ACT.Copy)
            nc.scalar.activation(second[:], y_rows[t][:].indirect(n2_t[:]), ACT.Copy)
            own = h_rows[t][:, S:]
            nc.scalar.activation(own, bank[:], ACT.Copy, scale=gn_neg[:, t : t + 1])
            larger = sb("larger%d" % t, [P, S], F32)
            nc.vector.tensor_tensor(larger[:], first[:], second[:], ALU.max)
            nc.vector.scalar_tensor_tensor(z_planes[:, t, :], larger[:], gn_t[:, t : t + 1], own, ALU.mult, ALU.add)

        def make_z2(t):
            bank = psum.tile([P, S], F32, name="s_bank%d" % t, tag="shared%d" % t)
            product(bank, (key_codes, key_scales), t, (x2_codes, x2_scales), True, True)
            s_rows = sb("s_rows%d" % t, [P, S], F32, ["w1_raw0", "pa0", "size0", "size1"][t])
            nc.scalar.activation(s_rows[:], bank[:], ACT.Copy, scale=0.0625)
            pa = sb("pa%d" % t, [P, W], F32)
            nc.scalar.activation(pa[:], s_rows[:].indirect(n4_t[:]), ACT.Copy)
            size = sb("size%d" % t, [P, W], F32)
            nc.scalar.activation(size[:], pa[:], ACT.Abs)
            root = sb("root%d" % t, [P, W], F32)
            nc.scalar.activation(root[:], size[:], ACT.Abs_reciprocal_sqrt, bias=0.5)
            half = sb("half%d" % t, [P, W], F32)
            nc.vector.tensor_tensor(half[:], s_rows[:].indirect(n3_t[:]), root[:], ALU.mult)
            nc.vector.tensor_tensor(s_rows[:].indirect(n3_t[:]), half[:], root[:], ALU.mult)
            nc.vector.tensor_scalar(z2_planes[:, t, :], s_rows[:], gk_t[:, t : t + 1], None, ALU.mult)

        make_z2(0)
        make_z2(1)
        make_z2(2)
        make_z(0)
        make_z2(3)
        z2_q = quantize("z2", interleave("z2_bf16", z2_planes, [nc.vector.tensor_copy], [S // PACK]))
        for t in range(1, PACK):
            make_z(t)
        w2_q = quantize("w2", round_weight("w2", w2_raw, [nc.scalar.copy], "y_rows3"))
        z_q = quantize("z", interleave("z_bf16", z_planes, [nc.vector.tensor_copy], [S // PACK]))
        h_banks = [psum.tile([P, S], F32, name="h_bank%d" % t, tag="last%d" % t) for t in range(PACK)]

        out_rows = out.rearrange("(p t) j -> p t j", t=PACK)
        for t in range(PACK):
            product(h_banks[t], w3_q, t, z2_q, True, False)
            product(h_banks[t], w2_q, t, z_q, False, True)
        for t in range(PACK):
            h = h_rows[t][:, :S]
            nc.vector.tensor_copy(h, h_banks[t][:])
            sg = sg_rows[t][:, :S]
            nc.scalar.activation(
                sg, h_rows[t][:].indirect(n5_t[:]), ACT.Sigmoid, bias=bias[:, t : t + 1], scale=sl_t[:, t : t + 1]
            )
            diff = sb("diff%d" % t, [P, S], F32)
            result = sb("result%d" % t, [P, S], F32)
            pieces = 2 if t == PACK - 1 else 1
            if t < 2:
                minus = sb("minus%d" % t, [P, S], F32)
                nc.vector.tensor_scalar(minus[:], sg, -1.0, None, ALU.mult)
                nc.vector.tensor_tensor(diff[:], sg_rows[t][:].indirect(n6_t[:]), minus[:], ALU.add)
            else:
                other = sb("other%d" % t, [P, S], F32)
            for piece in range(pieces):
                cols = slice(piece * S // pieces, (piece + 1) * S // pieces)
                if t >= 2:
                    entries = n6_t[:, cols.start // 16 : cols.stop // 16]
                    nc.scalar.activation(other[:, cols], sg_rows[t][:].indirect(entries), ACT.Copy)
                    nc.vector.tensor_tensor(diff[:, cols], other[:, cols], sg[:, cols], ALU.subtract)
                nc.vector.scalar_tensor_tensor(result[:, cols], h[:, cols], -1.5, diff[:, cols], ALU.mult, ALU.mult)
                nc.sync.dma_start(out_rows[:, t, cols], result[:, cols])
